import numpy as np
import ml_dtypes


def mxq(x, axis, fmt="e4m3"):
    dtype, down = {"e4m3": (ml_dtypes.float8_e4m3fn, 7), "e5m2": (ml_dtypes.float8_e5m2, 14)}[fmt]
    v = np.moveaxis(np.asarray(x, np.float32).astype(ml_dtypes.bfloat16).astype(np.float64), axis, -1)
    blocks = v.reshape(v.shape[:-1] + (-1, 32))
    amax = np.abs(blocks).max(-1, keepdims=True)
    byte = np.maximum(np.where(amax > 0, np.frexp(amax)[1] - 1 + 127, 0) - down, 1)
    scale = np.exp2(byte - 127.0)
    codes = (blocks / scale).astype(np.float32).astype(dtype).astype(np.float64)
    return np.moveaxis((codes * scale).reshape(v.shape), -1, axis)


WIDE = False


def mx_kscale(k):
    if not WIDE:
        return np.ones(k)
    levels = np.array([10, -10, 5, -5, 0])
    if k % 512:
        return np.exp2(np.random.permutation(np.resize(levels, k // 32))).repeat(32)
    a = np.empty((k // 512, 16))
    for p in range(k // 512):
        a[p, :8] = np.random.permutation(np.resize(levels, 8))
        for g in range(8):
            far = levels[np.abs(levels - a[p, g]) >= 10]
            a[p, g + 8] = far[np.random.randint(len(far))]
    return np.exp2(a.ravel()).repeat(32)


def f64(x):
    return np.asarray(x).astype(np.float64)


def striped(idx):
    return np.tile(idx.reshape(-1, 16).T, (8, 1)).astype(np.uint16)


def unstriped(offs):
    return offs[:16].T.reshape(-1).astype(np.int64)


def striped8(idx):
    return np.concatenate([x.reshape(-1, 16).T for x in idx]).astype(np.uint16)


def runs(offs, k):
    lists = np.stack([offs[16 * r : 16 * r + 16].T.reshape(-1) for r in range(8)]).astype(np.int64)
    return lists[np.arange(k) % 512 // 64]


def pack_weight(w):
    k, n = w.shape
    w = f64(np.asarray(w, np.float32).astype(ml_dtypes.bfloat16)).reshape(k // 32, 32, n)
    amax = np.abs(w).max(1)
    byte = np.clip(np.where(amax > 0, np.frexp(amax)[1] - 1 + 127 - 7, 1), 1, 254)
    scaled = (w * np.exp2(127.0 - byte)[:, None, :]).reshape(k, n).astype(np.float32)
    words = np.ascontiguousarray(scaled.reshape(k // 512, 128, 4, n).transpose(0, 1, 3, 2)).astype(ml_dtypes.float8_e4m3fn).view(np.uint8)
    return words, np.ascontiguousarray(byte.astype(np.uint8).reshape(k // 512, 16, n))


def unpack_weight(words, scales):
    g, p, n, _ = words.shape
    vals = np.ascontiguousarray(words).view(ml_dtypes.float8_e4m3fn).astype(np.float64) * np.repeat(np.exp2(scales.astype(np.float64) - 127.0), 8, axis=1)[..., None]
    return vals.transpose(0, 1, 3, 2).reshape(g * 512, n)


E2M1 = np.array([0.0, 0.5, 1.0, 1.5, 2.0, 3.0, 4.0, 6.0, -0.0, -0.5, -1.0, -1.5, -2.0, -3.0, -4.0, -6.0])


def pack_fp4(w):
    k, n = w.shape
    w = f64(np.asarray(w, np.float32).astype(ml_dtypes.bfloat16)).reshape(k // 32, 32, n)
    amax = np.abs(w).max(1)
    mant, ex = np.frexp(amax / 6.0)
    byte = np.clip(np.where(amax > 0, np.where(mant > 0.5, ex, ex - 1) + 127, 1), 1, 254)
    scaled = (w * np.exp2(127.0 - byte)[:, None, :]).reshape(k, n).astype(np.float32)
    c = np.ascontiguousarray(scaled.reshape(k // 512, 128, 4, n).transpose(0, 1, 3, 2)).astype(ml_dtypes.float4_e2m1fn).view(np.uint8) & 0xF
    words = (c[..., 0::2] | (c[..., 1::2] << 4)).reshape(k // 512, 128, 2 * n)
    return np.ascontiguousarray(words), np.ascontiguousarray(byte.astype(np.uint8).reshape(k // 512, 16, n))


def unpack_fp4(words, scales):
    g, _, n = scales.shape
    words = np.ascontiguousarray(words).reshape(g, 128, n, 2)
    nib = np.empty((g, 128, n, 4), np.uint8)
    nib[..., 0::2] = words & 0xF
    nib[..., 1::2] = words >> 4
    vals = E2M1[nib] * np.repeat(np.exp2(scales.astype(np.float64) - 127.0), 8, axis=1)[..., None]
    return vals.transpose(0, 1, 3, 2).reshape(g * 512, n)


K, T, S, H, G, U = 512, 2048, 256, 512, 2048, 512


def setup_inputs():
    n = np.random.standard_normal
    s = mx_kscale(K)[:, None]
    packed_xT = pack_weight(n((K, T)) * s)
    packed_w1 = pack_fp4(n((K, H)) / np.sqrt(K) / s)
    packed_dT = pack_weight(n((K, G)) / s)
    perm = np.random.permutation(U)
    return {
        "x_words": packed_xT[0],
        "x_scales": packed_xT[1],
        "w1_words": packed_w1[0],
        "w1_scales": packed_w1[1],
        "gs": (np.random.uniform(0.5, 1.5, (K, 1)) * s).astype(np.float32),
        "d_words": packed_dT[0],
        "d_scales": packed_dT[1],
        "offs": striped8(np.random.randint(0, T, (8, S))),
        "k1": striped8(np.random.randint(0, G, (8, H))),
        "n1": striped(perm[:S]),
        "n2": striped(perm[S:]),
        "n3": striped(np.random.permutation(S)),
    }


def reference(x_words, x_scales, w1_words, w1_scales, gs, d_words, d_scales, offs, k1, n1, n2, n3):
    d_k1 = unpack_weight(d_words, d_scales)[np.arange(K)[:, None], runs(k1, K)]
    xq = unpack_weight(x_words, x_scales)[np.arange(K)[:, None], runs(offs, K)]
    y = unpack_fp4(w1_words, w1_scales).T @ xq
    z = f64(gs) * y
    h = 0.0625 * ((d_k1.T @ mxq(z, 0, "e4m3")))
    nw = h - h[:, unstriped(n3)]
    ph = np.zeros((H, U))
    ph[:, unstriped(n1)] = h
    out = ph.copy()
    out[:, unstriped(n2)] = nw
    return out

@@ -1,0 +1,148 @@
+from contextlib import ExitStack
+
+import concourse.mybir as mybir
+
+K, T, S, H, G, U = 512, 2048, 256, 512, 2048, 512
+FLOPS = 2 * K * H * S + 2 * K * H * S
+
+F32 = mybir.dt.float32
+BF16 = mybir.dt.bfloat16
+I32 = mybir.dt.int32
+U32 = mybir.dt.uint32
+U16 = mybir.dt.uint16
+U8 = mybir.dt.uint8
+FP8X4 = mybir.dt.float8_e4m3fn_x4
+FP4X4 = mybir.dt.float4_e2m1fn_x4
+COPY = mybir.ActivationFunctionType.Copy
+MULT = mybir.AluOpType.mult
+SUB = mybir.AluOpType.subtract
+
+P = 128
+PACK = 4
+HALF = S // 2
+SPARE = 8
+
+
+def tile_picked_hdenseipagq_none_p_kernel(
+    tc, x_words, x_scales, w1_words, w1_scales, gs, d_words, d_scales, offs, k1, n1, n2, n3, out
+):
+    nc = tc.nc
+    with ExitStack() as ctx:
+        lists = ctx.enter_context(tc.tile_pool(name="lists", bufs=1))
+        keep = ctx.enter_context(tc.tile_pool(name="keep", bufs=1))
+        psum = ctx.enter_context(tc.psum_pool(name="psum", bufs=1))
+
+        offs_t = lists.tile([P, S // 16], U16, name="offs_t")
+        k1_t = lists.tile([P, H // 16], U16, name="k1_t")
+        n1_t = lists.tile([P, S // 16], U16, name="n1_t")
+        n2_t = lists.tile([P, S // 16], U16, name="n2_t")
+        n3_t = lists.tile([P, S // 16], U16, name="n3_t")
+
+        w1s_raw = keep.tile([P, H], U8, name="w1s_raw", align_bytes=64)
+        xs_table = keep.tile([P, T], U8, name="xs_table", align_bytes=64)
+        ds_table = keep.tile([P, G], U8, name="ds_table", align_bytes=64)
+        xw_table = keep.tile([P, T], U32, name="xw_table", align_bytes=64)
+        dw_table = keep.tile([P, G], U32, name="dw_table", align_bytes=64)
+        w1w_raw = keep.tile([P, H], U16, name="w1w_raw", align_bytes=64)
+        gs_t = keep.tile([P, PACK], F32, name="gs_t", align_bytes=64)
+
+        nc.vector.memset(w1s_raw[:].bitcast(I32), 0)
+        nc.vector.memset(xs_table[:].bitcast(I32), 0)
+        nc.vector.memset(ds_table[:].bitcast(I32), 0)
+
+        nc.sync.dma_start(offs_t[:], offs)
+        nc.sync.dma_start(k1_t[:], k1)
+        nc.scalar.dma_start(gs_t[:], gs.rearrange("(p t) o -> p (t o)", t=PACK))
+        nc.scalar.dma_start(w1w_raw[:].bitcast(I32), w1_words[0].bitcast(I32))
+        nc.sync.dma_start(w1s_raw[0:P:8, :].bitcast(I32), w1_scales[0].bitcast(I32))
+        nc.sync.dma_start(xs_table[0:P:8, :].bitcast(I32), x_scales[0].bitcast(I32))
+        nc.sync.dma_start(ds_table[0:P:8, :].bitcast(I32), d_scales[0].bitcast(I32))
+        nc.sync.dma_start(xw_table[:].bitcast(I32), x_words[0].rearrange("p n t -> p (n t)").bitcast(I32))
+        nc.sync.dma_start(n1_t[:], n1)
+        nc.sync.dma_start(n3_t[:], n3)
+        nc.sync.dma_start(n2_t[:], n2)
+        nc.sync.dma_start(dw_table[:].bitcast(I32), d_words[0].rearrange("p n t -> p (n t)").bitcast(I32))
+
+        h_tiles = [keep.tile([P, S + SPARE], F32, name=f"h{b}", align_bytes=64) for b in range(4)]
+        for b in range(4):
+            nc.gpsimd.memset(h_tiles[b][:, S:], 0.0)
+
+        w1w = keep.tile([P, PACK, P], U16, name="w1w", align_bytes=64)
+        nc.scalar.copy(w1w[:], w1w_raw[:].rearrange("p (m t) -> p t m", t=PACK))
+
+        plane1 = keep.tile([P, H + S], U8, name="plane1", align_bytes=64)
+        nc.vector.tensor_copy(
+            plane1[:, 0:H].rearrange("p (t m) -> p t m", t=PACK), w1s_raw[:].rearrange("p (m t) -> p t m", t=PACK)
+        )
+        xs_picked = keep.tile([P, S], U8, name="xs_picked", align_bytes=64)
+        nc.vector.tensor_copy(xs_picked[:], xs_table[:].indirect(offs_t[:]))
+        nc.vector.tensor_copy(plane1[:, H:].bitcast(I32), xs_picked[:].bitcast(I32))
+        for i in range(1, 4):
+            nc.scalar.dma_start(plane1[i:P:32, :].bitcast(I32), plane1[8 * i : P : 32, :].bitcast(I32))
+
+        ds_picked = keep.tile([P, H], U8, name="ds_picked", align_bytes=64)
+        nc.vector.tensor_copy(ds_picked[:], ds_table[:].indirect(k1_t[:]))
+        plane2 = keep.tile([P, H], U8, name="plane2", align_bytes=64)
+        nc.vector.tensor_copy(plane2[:].bitcast(I32), ds_picked[:].bitcast(I32))
+        for i in range(1, 4):
+            nc.scalar.dma_start(plane2[i:P:32, :].bitcast(I32), ds_picked[8 * i : P : 32, :].bitcast(I32))
+
+        xw_picked = keep.tile([P, S], U32, name="xw_picked", align_bytes=64)
+        nc.vector.tensor_copy(xw_picked[:], xw_table[:].indirect(offs_t[:]))
+
+        z_bf = keep.tile([P, S, PACK], BF16, name="z_bf", align_bytes=64)
+        for a in range(2):
+            cols = slice(a * HALF, (a + 1) * HALF)
+            y_ps = psum.tile([P, PACK, HALF], F32, name=f"y{a}")
+            for t in range(PACK):
+                nc.tensor.matmul_mx(
+                    out=y_ps[:, t, :],
+                    lhsT=w1w[:, t, :].bitcast(FP4X4),
+                    lhsT_scale=plane1[:, t * P : (t + 1) * P],
+                    rhs=xw_picked[:, cols].bitcast(FP8X4),
+                    rhs_scale=plane1[:, H + a * HALF : H + (a + 1) * HALF],
+                    start=True,
+                    stop=True,
+                )
+            nc.vector.tensor_tensor(
+                z_bf[:, cols, :],
+                y_ps[:].rearrange("p t n -> p n t"),
+                gs_t[:].unsqueeze(1).to_broadcast([P, HALF, PACK]),
+                MULT,
+            )
+        z_words = keep.tile([P, S], U32, name="z_words", align_bytes=64)
+        z_plane = keep.tile([P, S], U8, name="z_plane", align_bytes=64)
+        nc.vector.quantize_mx(
+            out=z_words[:].bitcast(FP8X4), scales=z_plane[:], in_=z_bf[:].rearrange("p n t -> p (n t)")
+        )
+
+        dw_picked = [keep.tile([P, H // 2], U32, name=f"dw_picked{c}", align_bytes=64) for c in range(2)]
+        for c in range(2):
+            nc.vector.tensor_copy(dw_picked[c][:], dw_table[:].indirect(k1_t[:, c * 16 : (c + 1) * 16]))
+            for b in (2 * c, 2 * c + 1):
+                h_ps = psum.tile([P, S], F32, name=f"hps{b}")
+                nc.tensor.matmul_mx(
+                    out=h_ps[:],
+                    lhsT=dw_picked[c][:, (b % 2) * P : (b % 2 + 1) * P].bitcast(FP8X4),
+                    lhsT_scale=plane2[:, b * P : (b + 1) * P],
+                    rhs=z_words[:].bitcast(FP8X4),
+                    rhs_scale=z_plane[:],
+                    start=True,
+                    stop=True,
+                )
+                h = h_tiles[b]
+                if b == 0:
+                    nc.scalar.activation(h[:, 0:S], h_ps[:], COPY, scale=0.0625)
+                else:
+                    nc.vector.tensor_scalar(h[:, 0:S], h_ps[:], 0.0625, None, MULT)
+
+        for b in range(4):
+            h = h_tiles[b]
+            looked = keep.tile([P, S], F32, name=f"looked{b}", align_bytes=64)
+            step = keep.tile([P, S], F32, name=f"step{b}", align_bytes=64)
+            page = keep.tile([P, U], F32, name=f"page{b}", align_bytes=64)
+            nc.scalar.activation(looked[:], h[:].indirect(n3_t[:]), COPY)
+            nc.vector.tensor_tensor(step[:], h[:, 0:S], looked[:], SUB)
+            nc.scalar.activation(page[:].indirect(n1_t[:]), h[:, 0:S], COPY)
+            nc.scalar.activation(page[:].indirect(n2_t[:]), step[:], COPY)
+            nc.sync.dma_start(out[b * P : (b + 1) * P, :], page[:])

@@ -30,6 +30,7 @@ def tile_picked_hdenseipagq_none_p_kernel(
     with ExitStack() as ctx:
         lists = ctx.enter_context(tc.tile_pool(name="lists", bufs=1))
         keep = ctx.enter_context(tc.tile_pool(name="keep", bufs=1))
+        reuse = ctx.enter_context(tc.tile_pool(name="reuse", bufs=1))
         psum = ctx.enter_context(tc.psum_pool(name="psum", bufs=1))
 
         offs_t = lists.tile([P, S // 16], U16, name="offs_t")
@@ -42,107 +43,135 @@ def tile_picked_hdenseipagq_none_p_kernel(
         xs_table = keep.tile([P, T], U8, name="xs_table", align_bytes=64)
         ds_table = keep.tile([P, G], U8, name="ds_table", align_bytes=64)
         xw_table = keep.tile([P, T], U32, name="xw_table", align_bytes=64)
-        dw_table = keep.tile([P, G], U32, name="dw_table", align_bytes=64)
         w1w_raw = keep.tile([P, H], U16, name="w1w_raw", align_bytes=64)
         gs_t = keep.tile([P, PACK], F32, name="gs_t", align_bytes=64)
 
-        nc.vector.memset(w1s_raw[:].bitcast(I32), 0)
         nc.vector.memset(xs_table[:].bitcast(I32), 0)
+        nc.vector.memset(w1s_raw[:].bitcast(I32), 0)
         nc.vector.memset(ds_table[:].bitcast(I32), 0)
 
         nc.sync.dma_start(offs_t[:], offs)
         nc.sync.dma_start(k1_t[:], k1)
-        nc.scalar.dma_start(gs_t[:], gs.rearrange("(p t) o -> p (t o)", t=PACK))
-        nc.scalar.dma_start(w1w_raw[:].bitcast(I32), w1_words[0].bitcast(I32))
-        nc.sync.dma_start(w1s_raw[0:P:8, :].bitcast(I32), w1_scales[0].bitcast(I32))
+        nc.sync.dma_start(w1w_raw[:].bitcast(I32), w1_words[0].bitcast(I32))
+        nc.sync.dma_start(gs_t[:], gs.rearrange("(p t) o -> p (t o)", t=PACK))
         nc.sync.dma_start(xs_table[0:P:8, :].bitcast(I32), x_scales[0].bitcast(I32))
+        nc.sync.dma_start(w1s_raw[0:P:8, :].bitcast(I32), w1_scales[0].bitcast(I32))
         nc.sync.dma_start(ds_table[0:P:8, :].bitcast(I32), d_scales[0].bitcast(I32))
         nc.sync.dma_start(xw_table[:].bitcast(I32), x_words[0].rearrange("p n t -> p (n t)").bitcast(I32))
         nc.sync.dma_start(n1_t[:], n1)
         nc.sync.dma_start(n3_t[:], n3)
         nc.sync.dma_start(n2_t[:], n2)
-        nc.sync.dma_start(dw_table[:].bitcast(I32), d_words[0].rearrange("p n t -> p (n t)").bitcast(I32))
 
         h_tiles = [keep.tile([P, S + SPARE], F32, name=f"h{b}", align_bytes=64) for b in range(4)]
         for b in range(4):
-            nc.gpsimd.memset(h_tiles[b][:, S:], 0.0)
+            nc.vector.memset(h_tiles[b][:, S:], 0.0)
 
         w1w = keep.tile([P, PACK, P], U16, name="w1w", align_bytes=64)
         nc.scalar.copy(w1w[:], w1w_raw[:].rearrange("p (m t) -> p t m", t=PACK))
 
         plane1 = keep.tile([P, H + S], U8, name="plane1", align_bytes=64)
+        xs_picked = reuse.tile([P, S], U8, name="xs_picked", offset=4 * G - S // 2, align_bytes=64)
+        nc.vector.tensor_copy(xs_picked[:], xs_table[:].indirect(offs_t[:]))
         nc.vector.tensor_copy(
             plane1[:, 0:H].rearrange("p (t m) -> p t m", t=PACK), w1s_raw[:].rearrange("p (m t) -> p t m", t=PACK)
         )
-        xs_picked = keep.tile([P, S], U8, name="xs_picked", align_bytes=64)
-        nc.vector.tensor_copy(xs_picked[:], xs_table[:].indirect(offs_t[:]))
         nc.vector.tensor_copy(plane1[:, H:].bitcast(I32), xs_picked[:].bitcast(I32))
-        for i in range(1, 4):
-            nc.scalar.dma_start(plane1[i:P:32, :].bitcast(I32), plane1[8 * i : P : 32, :].bitcast(I32))
+        for i, queue in ((1, nc.sync), (2, nc.scalar), (3, nc.sync)):
+            queue.dma_start(plane1[i:P:32, :].bitcast(I32), plane1[8 * i : P : 32, :].bitcast(I32))
+        dw_table = reuse.tile([P, G], U32, name="dw_table", offset=0, align_bytes=64)
+        nc.sync.dma_start(dw_table[:].bitcast(I32), d_words[0].rearrange("p n t -> p (n t)").bitcast(I32))
 
-        ds_picked = keep.tile([P, H], U8, name="ds_picked", align_bytes=64)
+        ds_picked = reuse.tile([P, H], U8, name="ds_picked", offset=4 * G, align_bytes=64)
         nc.vector.tensor_copy(ds_picked[:], ds_table[:].indirect(k1_t[:]))
         plane2 = keep.tile([P, H], U8, name="plane2", align_bytes=64)
         nc.vector.tensor_copy(plane2[:].bitcast(I32), ds_picked[:].bitcast(I32))
         for i in range(1, 4):
-            nc.scalar.dma_start(plane2[i:P:32, :].bitcast(I32), ds_picked[8 * i : P : 32, :].bitcast(I32))
+            nc.sync.dma_start(plane2[i:P:32, :].bitcast(I32), ds_picked[8 * i : P : 32, :].bitcast(I32))
 
         xw_picked = keep.tile([P, S], U32, name="xw_picked", align_bytes=64)
         nc.vector.tensor_copy(xw_picked[:], xw_table[:].indirect(offs_t[:]))
 
-        z_bf = keep.tile([P, S, PACK], BF16, name="z_bf", align_bytes=64)
-        for a in range(2):
-            cols = slice(a * HALF, (a + 1) * HALF)
+        z_words = keep.tile([P, S], U32, name="z_words", align_bytes=64)
+        z_plane = keep.tile([P, S], U8, name="z_plane", align_bytes=64)
+        halves = [slice(a * HALF, (a + 1) * HALF) for a in range(2)]
+        z_bf = keep.tile([P, S, PACK], BF16, name="z_bf", tag="z_then_dw", align_bytes=64)
+
+        def first_product(a):
             y_ps = psum.tile([P, PACK, HALF], F32, name=f"y{a}")
             for t in range(PACK):
                 nc.tensor.matmul_mx(
                     out=y_ps[:, t, :],
                     lhsT=w1w[:, t, :].bitcast(FP4X4),
                     lhsT_scale=plane1[:, t * P : (t + 1) * P],
-                    rhs=xw_picked[:, cols].bitcast(FP8X4),
+                    rhs=xw_picked[:, halves[a]].bitcast(FP8X4),
                     rhs_scale=plane1[:, H + a * HALF : H + (a + 1) * HALF],
                     start=True,
                     stop=True,
                 )
             nc.vector.tensor_tensor(
-                z_bf[:, cols, :],
+                z_bf[:, halves[a], :],
                 y_ps[:].rearrange("p t n -> p n t"),
                 gs_t[:].unsqueeze(1).to_broadcast([P, HALF, PACK]),
                 MULT,
             )
-        z_words = keep.tile([P, S], U32, name="z_words", align_bytes=64)
-        z_plane = keep.tile([P, S], U8, name="z_plane", align_bytes=64)
+
+        def pick_d_words(c, tag):
+            picked = keep.tile([P, H // 2], U32, name=f"dw_picked{c}", tag=tag, align_bytes=64)
+            nc.vector.tensor_copy(picked[:], dw_table[:].indirect(k1_t[:, c * 16 : (c + 1) * 16]))
+            return picked
+
+        def second_product(picked, b, cols):
+            h_ps = psum.tile([P, cols.stop - cols.start], F32, name=f"hps{b}_{cols.start}")
+            nc.tensor.matmul_mx(
+                out=h_ps[:],
+                lhsT=picked[:, (b % 2) * P : (b % 2 + 1) * P].bitcast(FP8X4),
+                lhsT_scale=plane2[:, b * P : (b + 1) * P],
+                rhs=z_words[:, cols].bitcast(FP8X4),
+                rhs_scale=z_plane[:, cols],
+                start=True,
+                stop=True,
+            )
+            return h_ps
+
+        page = [keep.tile([P, U], F32, name=f"page{b}", align_bytes=64) for b in range(4)]
+
+        def put_h(b, cols):
+            nc.scalar.activation(
+                page[b][:].indirect(n1_t[:, cols.start // 16 : cols.stop // 16]), h_tiles[b][:, cols], COPY
+            )
+
+        every = slice(0, S)
+        first_product(0)
+        first_product(1)
         nc.vector.quantize_mx(
             out=z_words[:].bitcast(FP8X4), scales=z_plane[:], in_=z_bf[:].rearrange("p n t -> p (n t)")
         )
+        picked = pick_d_words(0, "dw_first")
+        h_ps = second_product(picked, 0, halves[0])
+        nc.scalar.activation(h_tiles[0][:, halves[0]], h_ps[:], COPY, scale=0.0625)
+        put_h(0, halves[0])
+        for b, cols in ((0, halves[1]), (1, every)):
+            h_ps = second_product(picked, b, cols)
+            nc.vector.tensor_scalar(h_tiles[b][:, cols], h_ps[:], 0.0625, None, MULT)
+        picked = pick_d_words(1, "z_then_dw")
+        for b in (2, 3):
+            h_ps = second_product(picked, b, every)
+            nc.vector.tensor_scalar(h_tiles[b][:, every], h_ps[:], 0.0625, None, MULT)
 
-        dw_picked = [keep.tile([P, H // 2], U32, name=f"dw_picked{c}", align_bytes=64) for c in range(2)]
-        for c in range(2):
-            nc.vector.tensor_copy(dw_picked[c][:], dw_table[:].indirect(k1_t[:, c * 16 : (c + 1) * 16]))
-            for b in (2 * c, 2 * c + 1):
-                h_ps = psum.tile([P, S], F32, name=f"hps{b}")
-                nc.tensor.matmul_mx(
-                    out=h_ps[:],
-                    lhsT=dw_picked[c][:, (b % 2) * P : (b % 2 + 1) * P].bitcast(FP8X4),
-                    lhsT_scale=plane2[:, b * P : (b + 1) * P],
-                    rhs=z_words[:].bitcast(FP8X4),
-                    rhs_scale=z_plane[:],
-                    start=True,
-                    stop=True,
-                )
-                h = h_tiles[b]
-                if b == 0:
-                    nc.scalar.activation(h[:, 0:S], h_ps[:], COPY, scale=0.0625)
-                else:
-                    nc.vector.tensor_scalar(h[:, 0:S], h_ps[:], 0.0625, None, MULT)
+        looked = [keep.tile([P, S], F32, name=f"looked{b}", align_bytes=64) for b in range(4)]
+        step = [keep.tile([P, S], F32, name=f"step{b}", align_bytes=64) for b in range(4)]
+
+        def look_up(b):
+            nc.scalar.activation(looked[b][:], h_tiles[b][:].indirect(n3_t[:]), COPY)
+            nc.vector.tensor_tensor(step[b][:], h_tiles[b][:, 0:S], looked[b][:], SUB)
+
+        def put_step(b):
+            nc.scalar.activation(page[b][:].indirect(n2_t[:]), step[b][:], COPY)
+            nc.sync.dma_start(out[b * P : (b + 1) * P, :], page[b][:])
 
         for b in range(4):
-            h = h_tiles[b]
-            looked = keep.tile([P, S], F32, name=f"looked{b}", align_bytes=64)
-            step = keep.tile([P, S], F32, name=f"step{b}", align_bytes=64)
-            page = keep.tile([P, U], F32, name=f"page{b}", align_bytes=64)
-            nc.scalar.activation(looked[:], h[:].indirect(n3_t[:]), COPY)
-            nc.vector.tensor_tensor(step[:], h[:, 0:S], looked[:], SUB)
-            nc.scalar.activation(page[:].indirect(n1_t[:]), h[:, 0:S], COPY)
-            nc.scalar.activation(page[:].indirect(n2_t[:]), step[:], COPY)
-            nc.sync.dma_start(out[b * P : (b + 1) * P, :], page[:])
+            look_up(b)
+            put_h(b, every if b > 0 else halves[1])
+            if b > 0:
+                put_step(b - 1)
+        put_step(3)

@@ -143,9 +143,12 @@ def tile_picked_hdenseipagq_none_p_kernel(
         every = slice(0, S)
         first_product(0)
         first_product(1)
-        nc.vector.quantize_mx(
-            out=z_words[:].bitcast(FP8X4), scales=z_plane[:], in_=z_bf[:].rearrange("p n t -> p (n t)")
-        )
+        for cols in halves:
+            nc.vector.quantize_mx(
+                out=z_words[:, cols].bitcast(FP8X4),
+                scales=z_plane[:, cols],
+                in_=z_bf[:, cols, :].rearrange("p n t -> p (n t)"),
+            )
         picked = pick_d_words(0, "dw_first")
         h_ps = second_product(picked, 0, halves[0])
         nc.scalar.activation(h_tiles[0][:, halves[0]], h_ps[:], COPY, scale=0.0625)

from contextlib import ExitStack

import concourse.mybir as mybir

K, T, S, H, G, U = 512, 2048, 256, 512, 2048, 512
FLOPS = 2 * K * H * S + 2 * K * H * S

F32 = mybir.dt.float32
BF16 = mybir.dt.bfloat16
I32 = mybir.dt.int32
U32 = mybir.dt.uint32
U16 = mybir.dt.uint16
U8 = mybir.dt.uint8
FP8X4 = mybir.dt.float8_e4m3fn_x4
FP4X4 = mybir.dt.float4_e2m1fn_x4
COPY = mybir.ActivationFunctionType.Copy
MULT = mybir.AluOpType.mult
SUB = mybir.AluOpType.subtract

P = 128
PACK = 4
HALF = S // 2
SPARE = 8


def tile_picked_hdenseipagq_none_p_kernel(
    tc, x_words, x_scales, w1_words, w1_scales, gs, d_words, d_scales, offs, k1, n1, n2, n3, out
):
    nc = tc.nc
    with ExitStack() as ctx:
        lists = ctx.enter_context(tc.tile_pool(name="lists", bufs=1))
        keep = ctx.enter_context(tc.tile_pool(name="keep", bufs=1))
        reuse = ctx.enter_context(tc.tile_pool(name="reuse", bufs=1))
        psum = ctx.enter_context(tc.psum_pool(name="psum", bufs=1))

        offs_t = lists.tile([P, S // 16], U16, name="offs_t")
        k1_t = lists.tile([P, H // 16], U16, name="k1_t")
        n1_t = lists.tile([P, S // 16], U16, name="n1_t")
        n2_t = lists.tile([P, S // 16], U16, name="n2_t")
        n3_t = lists.tile([P, S // 16], U16, name="n3_t")

        w1s_raw = keep.tile([P, H], U8, name="w1s_raw", align_bytes=64)
        xs_table = keep.tile([P, T], U8, name="xs_table", align_bytes=64)
        ds_table = keep.tile([P, G], U8, name="ds_table", align_bytes=64)
        xw_table = keep.tile([P, T], U32, name="xw_table", align_bytes=64)
        w1w_raw = keep.tile([P, H], U16, name="w1w_raw", align_bytes=64)
        gs_t = keep.tile([P, PACK], F32, name="gs_t", align_bytes=64)

        nc.vector.memset(xs_table[:].bitcast(I32), 0)
        nc.vector.memset(w1s_raw[:].bitcast(I32), 0)
        nc.vector.memset(ds_table[:].bitcast(I32), 0)

        nc.sync.dma_start(offs_t[:], offs)
        nc.sync.dma_start(k1_t[:], k1)
        nc.sync.dma_start(w1w_raw[:].bitcast(I32), w1_words[0].bitcast(I32))
        nc.sync.dma_start(gs_t[:], gs.rearrange("(p t) o -> p (t o)", t=PACK))
        nc.sync.dma_start(xs_table[0:P:8, :].bitcast(I32), x_scales[0].bitcast(I32))
        nc.sync.dma_start(w1s_raw[0:P:8, :].bitcast(I32), w1_scales[0].bitcast(I32))
        nc.sync.dma_start(ds_table[0:P:8, :].bitcast(I32), d_scales[0].bitcast(I32))
        nc.sync.dma_start(xw_table[:].bitcast(I32), x_words[0].rearrange("p n t -> p (n t)").bitcast(I32))
        nc.sync.dma_start(n1_t[:], n1)
        nc.sync.dma_start(n3_t[:], n3)
        nc.sync.dma_start(n2_t[:], n2)

        h_tiles = [keep.tile([P, S + SPARE], F32, name=f"h{b}", align_bytes=64) for b in range(4)]
        for b in range(4):
            nc.vector.memset(h_tiles[b][:, S:], 0.0)

        w1w = keep.tile([P, PACK, P], U16, name="w1w", align_bytes=64)
        nc.scalar.copy(w1w[:], w1w_raw[:].rearrange("p (m t) -> p t m", t=PACK))

        plane1 = keep.tile([P, H + S], U8, name="plane1", align_bytes=64)
        xs_picked = reuse.tile([P, S], U8, name="xs_picked", offset=4 * G - S // 2, align_bytes=64)
        nc.vector.tensor_copy(xs_picked[:], xs_table[:].indirect(offs_t[:]))
        nc.vector.tensor_copy(
            plane1[:, 0:H].rearrange("p (t m) -> p t m", t=PACK), w1s_raw[:].rearrange("p (m t) -> p t m", t=PACK)
        )
        nc.vector.tensor_copy(plane1[:, H:].bitcast(I32), xs_picked[:].bitcast(I32))
        for i, queue in ((1, nc.sync), (2, nc.scalar), (3, nc.sync)):
            queue.dma_start(plane1[i:P:32, :].bitcast(I32), plane1[8 * i : P : 32, :].bitcast(I32))
        dw_table = reuse.tile([P, G], U32, name="dw_table", offset=0, align_bytes=64)
        nc.sync.dma_start(dw_table[:].bitcast(I32), d_words[0].rearrange("p n t -> p (n t)").bitcast(I32))

        ds_picked = reuse.tile([P, H], U8, name="ds_picked", offset=4 * G, align_bytes=64)
        nc.vector.tensor_copy(ds_picked[:], ds_table[:].indirect(k1_t[:]))
        plane2 = keep.tile([P, H], U8, name="plane2", align_bytes=64)
        nc.vector.tensor_copy(plane2[:].bitcast(I32), ds_picked[:].bitcast(I32))
        for i in range(1, 4):
            nc.sync.dma_start(plane2[i:P:32, :].bitcast(I32), ds_picked[8 * i : P : 32, :].bitcast(I32))

        xw_picked = keep.tile([P, S], U32, name="xw_picked", align_bytes=64)
        nc.vector.tensor_copy(xw_picked[:], xw_table[:].indirect(offs_t[:]))

        z_words = keep.tile([P, S], U32, name="z_words", align_bytes=64)
        z_plane = keep.tile([P, S], U8, name="z_plane", align_bytes=64)
        halves = [slice(a * HALF, (a + 1) * HALF) for a in range(2)]
        z_bf = keep.tile([P, S, PACK], BF16, name="z_bf", tag="z_then_dw", align_bytes=64)

        def first_product(a):
            y_ps = psum.tile([P, PACK, HALF], F32, name=f"y{a}")
            for t in range(PACK):
                nc.tensor.matmul_mx(
                    out=y_ps[:, t, :],
                    lhsT=w1w[:, t, :].bitcast(FP4X4),
                    lhsT_scale=plane1[:, t * P : (t + 1) * P],
                    rhs=xw_picked[:, halves[a]].bitcast(FP8X4),
                    rhs_scale=plane1[:, H + a * HALF : H + (a + 1) * HALF],
                    start=True,
                    stop=True,
                )
            nc.vector.tensor_tensor(
                z_bf[:, halves[a], :],
                y_ps[:].rearrange("p t n -> p n t"),
                gs_t[:].unsqueeze(1).to_broadcast([P, HALF, PACK]),
                MULT,
            )

        def pick_d_words(c, tag):
            picked = keep.tile([P, H // 2], U32, name=f"dw_picked{c}", tag=tag, align_bytes=64)
            nc.vector.tensor_copy(picked[:], dw_table[:].indirect(k1_t[:, c * 16 : (c + 1) * 16]))
            return picked

        def second_product(picked, b, cols):
            h_ps = psum.tile([P, cols.stop - cols.start], F32, name=f"hps{b}_{cols.start}")
            nc.tensor.matmul_mx(
                out=h_ps[:],
                lhsT=picked[:, (b % 2) * P : (b % 2 + 1) * P].bitcast(FP8X4),
                lhsT_scale=plane2[:, b * P : (b + 1) * P],
                rhs=z_words[:, cols].bitcast(FP8X4),
                rhs_scale=z_plane[:, cols],
                start=True,
                stop=True,
            )
            return h_ps

        page = [keep.tile([P, U], F32, name=f"page{b}", align_bytes=64) for b in range(4)]

        def put_h(b, cols):
            nc.scalar.activation(
                page[b][:].indirect(n1_t[:, cols.start // 16 : cols.stop // 16]), h_tiles[b][:, cols], COPY
            )

        every = slice(0, S)
        first_product(0)
        first_product(1)
        for cols in halves:
            nc.vector.quantize_mx(
                out=z_words[:, cols].bitcast(FP8X4),
                scales=z_plane[:, cols],
                in_=z_bf[:, cols, :].rearrange("p n t -> p (n t)"),
            )
        picked = pick_d_words(0, "dw_first")
        h_ps = second_product(picked, 0, halves[0])
        nc.scalar.activation(h_tiles[0][:, halves[0]], h_ps[:], COPY, scale=0.0625)
        put_h(0, halves[0])
        for b, cols in ((0, halves[1]), (1, every)):
            h_ps = second_product(picked, b, cols)
            nc.vector.tensor_scalar(h_tiles[b][:, cols], h_ps[:], 0.0625, None, MULT)
        picked = pick_d_words(1, "z_then_dw")
        for b in (2, 3):
            h_ps = second_product(picked, b, every)
            nc.vector.tensor_scalar(h_tiles[b][:, every], h_ps[:], 0.0625, None, MULT)

        looked = [keep.tile([P, S], F32, name=f"looked{b}", align_bytes=64) for b in range(4)]
        step = [keep.tile([P, S], F32, name=f"step{b}", align_bytes=64) for b in range(4)]

        def look_up(b):
            nc.scalar.activation(looked[b][:], h_tiles[b][:].indirect(n3_t[:]), COPY)
            nc.vector.tensor_tensor(step[b][:], h_tiles[b][:, 0:S], looked[b][:], SUB)

        def put_step(b):
            nc.scalar.activation(page[b][:].indirect(n2_t[:]), step[b][:], COPY)
            nc.sync.dma_start(out[b * P : (b + 1) * P, :], page[b][:])

        for b in range(4):
            look_up(b)
            put_h(b, every if b > 0 else halves[1])
            if b > 0:
                put_step(b - 1)
        put_step(3)
